import numpy as np, ml_dtypes
CORES = [16,17,18,19,32,33,34,35]
N = 8
import mx_ref
BF = ml_dtypes.bfloat16
def f(rng, *shape):
    return mx_ref.flush((rng.standard_normal(shape, dtype=np.float32) * np.exp2(rng.integers(-2, 3, shape[:-1] + (1,)))).astype(BF))
def wide(rng, *shape, cols=0):
    v = rng.standard_normal(shape, dtype=np.float32) * np.exp2(rng.integers(-12, 13, shape)).astype(np.float32)
    if cols: v *= np.repeat(np.exp2(rng.integers(-cols, cols + 1, shape[:-2] + (1, shape[-1] // 4))) * (rng.random(shape[:-2] + (1, shape[-1] // 4)) > 0.0625), 4, axis=-1).astype(np.float32)
    return mx_ref.flush(v.astype(BF))
def cols(t, e):
    v = np.concatenate([t.reshape(128, -1, 4), np.zeros((128, 1, 4), BF)], axis=1)
    return np.ascontiguousarray(v[:, e]).reshape(128, -1)
def tile(rs):
    return np.stack(rs, axis=2).reshape(128, -1).astype(BF)
def cut(t, i, w=512):
    return t[:, w * i:w * i + w]
def decode(q):
    o = []
    for b in range(4):
        e = np.zeros((128, 128, 4), np.float32); e[np.arange(128), np.arange(128), b] = 1
        o.append(mx_ref.matmul(mx_ref.quantize(e.reshape(128, 512).astype(BF)), q))
    return np.stack(o, axis=2).reshape(128, -1)
T, CK = 256, 48
def gates(g):
    t = np.zeros((128, 512), BF); t[:, :4 * N] = g
    return np.stack([t] * N)
def plus(g):
    return np.maximum(np.abs(g.astype(np.float32)), np.float32(0.0625)).astype(BF)
def apart(rng):
    g = np.zeros((128, 4 * N), BF)
    for e in range(N): g[8 * e:8 * e + 8, 4 * e:4 * e + 4] = plus(f(rng, 8, 4))
    return g
def setup_inputs(rng):
    return {"x": f(rng, N, 128, 4 * T), "wg": gates(f(rng, 128, 4 * N)), "w1": f(rng, N, 128, 2048)}
def setup_inputs_alike(rng):
    d = setup_inputs(rng); d["wg"] = gates(np.tile(f(rng, 128, 4), (1, N))); return d
def setup_inputs_ties(rng):
    d = setup_inputs(rng); d["wg"] = gates(plus(f(rng, 128, 4 * N))); d["x"] = -plus(d["x"])
    for s in range(N):
        k = rng.permutation(np.arange(T) // 5 if s % 2 else np.arange(T) % (T // (CK + 1)))
        d["x"][s] = d["x"][s].reshape(128, T, 4)[:, k].reshape(128, -1)
    return d
def setup_inputs_split(rng):
    d = setup_inputs(rng); g = apart(rng)
    v = d["x"].astype(np.float32).reshape(N, 128, T, 4)
    for s in range(N):
        p = rng.permutation(T)
        for e in range(N):
            sign = np.full((1, T, 1), -1, np.float32); sign[:, p[(e * CK + np.arange(CK)) % T]] = 1
            v[s, 8 * e:8 * e + 8] = np.abs(v[s, 8 * e:8 * e + 8]) * sign
    d["x"] = v.reshape(N, 128, 4 * T).astype(BF); d["wg"] = gates(g); return d
def setup_inputs_zeros(rng):
    d = setup_inputs(rng); g = apart(rng)
    v = d["x"].astype(np.float32).reshape(N, 128, T, 4)
    for s in range(N):
        for e in range(N):
            p = rng.permutation(T); u = np.abs(v[s, 8 * e:8 * e + 8])
            u[:, p[CK // 2:CK // 2 + CK]] = np.where(rng.random((8, CK, 4)) < 0.5, np.float32(-0.0), np.float32(0.0))
            u[:, p[CK // 2 + CK:]] *= np.float32(-1)
            v[s, 8 * e:8 * e + 8] = u
    d["x"] = v.reshape(N, 128, 4 * T).astype(BF); d["wg"] = gates(g); return d
def setup_inputs_spread(rng):
    d = setup_inputs(rng); d["x"] = wide(rng, N, 128, 4 * T, cols=6); return d
def check_inputs(d):
    b = []
    g = d["wg"].astype(np.float32)
    if (g != g[0]).any() or (g[:, :, 4 * N:] != 0).any(): b.append("wg")
    return b
def reference(x, wg, w1):
    took = []
    for s in range(N):
        z = mx_ref.matmul(mx_ref.quantize(wg[s]), mx_ref.quantize(x[s])) + np.float32(0.0)
        took.append([np.argsort(-z[e], kind="stable")[:CK] for e in range(N)])
    y = np.zeros((N, 128, T, 4), np.float32)
    for e in range(N):
        q = mx_ref.quantize(np.concatenate([cols(x[s], took[s][e]) for s in range(N)], axis=1))
        rs = [np.maximum(mx_ref.matmul(mx_ref.quantize(np.ascontiguousarray(cut(w1[e], i))), q), np.float32(0.0)) * np.float32(0.05) for i in range(4)]
        v = decode(mx_ref.quantize(tile(rs))).reshape(128, N, CK, 4)
        for s in range(N): y[s][:, took[s][e]] += v[:, s]
    return {"y": y.reshape(N, 128, 4 * T)}

@@ -1,0 +1,317 @@
+from concourse.bass import DstId, RemoteDMATransfer
+from concourse.mybir import dt, AluOpType as A, ActivationFunctionType as F
+
+CK = 48
+W4 = 4 * CK
+VB = [0, 1, 2, 3, 4]
+SB = [5, 6, 7]
+NV = len(VB)
+
+SCRATCH = {}
+
+
+def _sbuf(dtype, names):
+    for w in names.split():
+        n, c = w.split(":")
+        for m in ([n[:-1] + "0", n[:-1] + "1"] if n.endswith("@") else [n]):
+            SCRATCH[m] = ("sbuf", [128, int(c)], dtype)
+
+
+_sbuf("bfloat16", "wgs:32 xs:1024 w1s:2048 onesb:2048 eb:2048 d0blk:256 d0cnt:%d hf:768 hn:768 gt@:512 cmp@:%d cs@:%d sg@:%d eqb@:256 es@:256 xg@:768"
+      % (256 * NV, 256 * NV, 256 * NV, 256 * len(SB)))
+for _d, _s in (("float8_e4m3fn_x4", "q"), ("uint8", "c")):
+    _sbuf(_d, " ".join("%s%s%s" % (w[0], _s, w[1:]) for w in "x:256 w:512 e:512 t:192 r:192 n:336 h:192 d:192 m:336 g@:128".split()))
+_sbuf("int32", "ic:32 p3:32 ib:256 ibm:256 hi:8 qi:8")
+_sbuf("float32", "odd:4 even:4 h64:4 icol:4 mk:4 tok0:128 tokv:128 idr:384 pl:640 dg0:160 dg1:160 dg2:160 dg3:160 d01:160 d23:160 dd:160 dsb:1536 pb:1552 yt:1024")
+_sbuf("float32", "tt@:256 ac@:8 a2@:4 a3@:4 rk@:8 wn@:272 t2@:128 v4@:4 ua@:4 ub@:4 o3@:4 ob@:12")
+_sbuf("uint16", "op:160 go@:32 ru@:8 ol@:16 oa@:12 obb@:12 occ@:12 odd4@:12")
+for _b in range(8):
+    SCRATCH["ps%d" % _b] = ("psum", [128, 512], "float32")
+
+SEMAPHORES = ["v", "t", "s", "p", "dwg", "dx", "dw", "lo0", "lo1", "af", "an", "rf", "rn", "ls", "dy"]
+
+
+def rank_program(g, core, T, topo):
+    rank = T.rank_of(core)
+    if rank is None:
+        return
+    N = len(T.cores)
+    near_of = lambda r: [k for k in range(N) if k != r and topo.chip(T.cores[k]) == topo.chip(T.cores[r])]
+    far_of = lambda r: [k for k in range(N) if topo.chip(T.cores[k]) != topo.chip(T.cores[r])]
+    others, far = near_of(rank), far_of(rank)
+    X = [far, others + [rank]]
+    where = {e: (h, a) for h in range(2) for a, e in enumerate(X[h])}
+    far_e = topo.engines(core, T.cores[far[0]])
+    near_e = [e for e in topo.engines(core, T.cores[others[0]]) if e not in far_e]
+
+    Q = {"v": g.vector, "t": g.tensor, "s": g.scalar, "p": g, "y": g.sync}
+    cnt = {"v": 0, "t": 0, "s": 0, "p": 0}
+    seen = {}
+
+    def need(q, *toks):
+        for s, n in toks:
+            if seen.get((q, s), 0) < n:
+                Q[q].wait_ge(T.sem[s], n)
+                seen[(q, s)] = n
+
+    def done(q, ins):
+        ins.then_inc(T.sem[q], 1)
+        cnt[q] += 1
+        return (q, cnt[q])
+
+    V, S, PE = g.vector, g.scalar, g.tensor
+    v = lambda ins: done("v", ins)
+    s = lambda ins: done("s", ins)
+    t = lambda ins: done("t", ins)
+    p = lambda ins: done("p", ins)
+    ts = lambda out, in0, s1, s2, *ops: v(V.tensor_scalar(out, in0, s1, s2, *ops))
+    tt = lambda out, a, b, op: v(V.tensor_tensor(out, a, b, op))
+
+    g.sync.dma_start(T.wgs[:], T.wg[:, 0:32]).then_inc(T.sem.dwg, 16)
+    g.sync.dma_start(T.xs[:, 0:512], T.x[:, 0:512]).then_inc(T.sem.dx, 16)
+    g.scalar.dma_start(T.xs[:, 512:1024], T.x[:, 512:1024]).then_inc(T.sem.dx, 16)
+    g.sync.dma_start(T.w1s[:], T.w1[:]).then_inc(T.sem.dw, 16)
+    DWG, DX, DW = ("dwg", 16), ("dx", 32), ("dw", 16)
+
+    p_ic = p(g.iota(T.ic[:], [[0, 32]], 0, 1))
+    p_ib = p(g.iota(T.ib[:], [[1, 256]], 128, -1))
+    p_tok = p(g.iota(T.tok0[:], [[128, 8], [4, 16]], 0, 0, allow_small_or_imprecise_dtypes=True))
+    v_ones = v(V.memset(T.onesb[:], 1.0))
+    need("p", v_ones)
+    p_eb = p(g.affine_select(T.eb[:], T.onesb[:], [[1, 4], [-1, 512]], A.is_equal, 0.0, 0, 4))
+    p_id = p(g.iota(T.idr[:], [[W4, N], [4, CK]], 16, 0, allow_small_or_imprecise_dtypes=True))
+    need("v", p_ic)
+    v_p3 = ts(T.p3[:], T.ic[:], 3, None, A.bitwise_and)
+    v_hi = ts(T.hi[:, 0:1], T.ic[:, 0:1], 4, 1, A.logical_shift_right, A.bitwise_and)
+    v_qi = ts(T.qi[:, 0:1], T.ic[:, 0:1], 2, 3, A.logical_shift_right, A.bitwise_and)
+    need("v", v_p3)
+    v_go = [None, None]
+    for h in range(2):
+        for a in range(4):
+            v_go[h] = ts(T["go%d" % h][:, 8 * a:8 * a + 8], T.p3[:, 8 * a:8 * a + 8], 4 * X[h][a], None, A.add)
+    s_gt = [None, None]
+    need("s", DWG)
+    for h in range(2):
+        need("s", v_go[h])
+        s_gt[h] = s(S.activation(T["gt%d" % h][:], T.wgs[:, 0:32].indirect(T["go%d" % h][:, 0:32]), F.Copy))
+    v_d1 = v(V.memset(T.d0cnt[:], 1.0))
+    need("v", v_hi, v_qi)
+    v_odd = ts(T.odd[:, 0:1], T.hi[:, 0:1], 1.0, None, A.mult)
+    v_h64 = ts(T.h64[:, 0:1], T.hi[:, 0:1], 64.0, None, A.mult)
+    v_even = ts(T.even[:, 0:1], T.hi[:, 0:1], -1.0, 1.0, A.mult, A.add)
+    need("v", p_ib)
+    v_ibm = ts(T.ibm[:], T.ib[:], 31, None, A.bitwise_and)
+    need("v", v_d1)
+    v_d0 = v(V.memset(T.d0cnt[:, 0:256 * NV:256], 0.0))
+    v_z = [v(V.memset(T["ac%d" % h][:], 0.0)) for h in range(2)]
+    need("v", v_h64, p_tok)
+    v_tok = ts(T.tokv[:], T.tok0[:], T.h64[:, 0:1], None, A.add)
+    v_wn = [v(V.memset(T.wn0[:], 0.0)), None]
+    need("v", v_ibm)
+    v_blk = ts(T.d0blk[:], T.ibm[:], 0, None, A.not_equal)
+
+    need("v", s_gt[0])
+    v_gq0 = v(V.quantize_mx(T.gq0[:, 0:128], T.gc0[:, 0:128], T.gt0[:, 0:512]))
+    need("v", DX)
+    v_xq = v(V.quantize_mx(T.xq[:, 0:256], T.xc[:, 0:256], T.xs[:, 0:1024]))
+    need("v", s_gt[1])
+    v_gq1 = v(V.quantize_mx(T.gq1[:, 0:128], T.gc1[:, 0:128], T.gt1[:, 0:512]))
+    sv, ss = [T.ps4, T.ps6], [T.ps5, T.ps7]
+    t_sv, t_ss = [None, None], [None, None]
+    for h in range(2):
+        need("t", v_xq, (v_gq0, v_gq1)[h])
+        mm = lambda out: t(PE.matmul_mx(out, T["gq%d" % h][:, 0:128], T["gc%d" % h][:, 0:128], T.xq[:, 0:256], T.xc[:, 0:256], True, True))
+        t_sv[h] = mm(sv[h][:, 0:256])
+        t_ss[h] = mm(ss[h][:, 0:256])
+
+    s_cnt, v_cnt, v_es, v_svread = [None, None], [None, None], [None, None], [None, None]
+
+    def count(h):
+        P, own, cm, PS, sg, ac = sv[h], T["tt%d" % h], T["cmp%d" % h], ss[h], T["sg%d" % h], T["ac%d" % h]
+        need("v", t_sv[h])
+        v_tt = v(V.transpose(own[:], P[:, 0:256]))
+        need("s", t_ss[h], v_tt, v_z[h])
+        sgn = [s(S.activation(sg[:, 256 * u:256 * u + 256], PS[:, 0:256], F.Sign, bias=own[:, 32 * b:32 * b + 1], scale=-1.0)) for u, b in enumerate(SB)]
+        for u, b in enumerate(SB):
+            need("s", sgn[u])
+            m = 256 * u + 32 * (b + 1)
+            lo, hi = sg[:, 256 * u:m], sg[:, m:256 * u + 256]
+            s_cnt[h] = s(S.activation(lo, lo, F.Sign, bias=1.0, scale=-2.0, accum_out=ac[:, u:u + 1]))
+            if b < 7:
+                s_cnt[h] = s(S.activation(hi, hi, F.Sign, bias=-1.0, scale=-2.0, accum_out=ac[:, 3 + u:4 + u]))
+        need("v", v_tt)
+        v_eq = tt(T["eqb%d" % h][:], P[:, 0:256], own[:], A.is_equal)
+        for u, b in enumerate(VB):
+            m = 32 * (b + 1)
+            ts(cm[:, 256 * u:256 * u + m], P[:, 0:m], own[:, 32 * b:32 * b + 1], None, A.is_ge)
+            v_svread[h] = ts(cm[:, 256 * u + m:256 * u + 256], P[:, m:256], own[:, 32 * b:32 * b + 1], None, A.is_gt)
+        need("v", v_eq, v_blk)
+        v_es[h] = v(V.tensor_tensor_scan(T["es%d" % h][:], T.d0blk[:], T["eqb%d" % h][:], 0.0, A.mult, A.add))
+        need("v", v_svread[h], v_d0)
+        v_cnt[h] = v(V.tensor_tensor_scan(T["cs%d" % h][:], T.d0cnt[:], cm[:], 0.0, A.mult, A.add))
+
+    v_o3 = [None, None]
+
+    def invert(h):
+        B = lambda n: T["%s%d" % (n, h)]
+        need("v", s_cnt[h])
+        x2 = tt(B("a2")[:, 0:3], B("ac")[:, 0:3], B("ac")[:, 3:6], A.add)
+        need("v", v_cnt[h], v_es[h])
+        tt(B("rk")[:, 0:NV], B("cs")[:, 255:256 * NV:256], B("es")[:, 31:32 * NV:32], A.subtract)
+        need("v", x2)
+        x3 = ts(B("a3")[:, 0:3], B("a2")[:, 0:3], 0.5, 128.0, A.mult, A.add)
+        need("v", x3)
+        r2 = tt(B("rk")[:, NV:8], B("a3")[:, 0:3], B("es")[:, 32 * NV + 31:256:32], A.subtract)
+        need("v", r2)
+        ru = ts(B("ru")[:, 0:8], B("rk")[:, 0:8], 16.0, None, A.add)
+        need("v", ru, v_tok, v_wn[h])
+        w = v(V.tensor_copy(B("wn")[:, 0:272].indirect(B("ru")[:, 0:8]), T.tokv[:, 0:128]))
+        need("v", w)
+        ta = v(V.transpose(B("t2")[:, 0:64], B("wn")[:, 0:64]))
+        tb = v(V.transpose(B("t2")[:, 64:128], B("wn")[:, 16:80]))
+        need("v", ta)
+        tt(B("v4")[:, 0:4:2], B("t2")[:, 0:64:32], B("t2")[:, 16:64:32], A.add)
+        need("v", tb)
+        vb = tt(B("v4")[:, 1:4:2], B("t2")[:, 64:128:32], B("t2")[:, 80:128:32], A.add)
+        need("v", vb, v_odd, v_even)
+        ts(B("ua")[:, 0:3], B("v4")[:, 0:3], T.odd[:, 0:1], None, A.mult)
+        ub = ts(B("ub")[:, 0:3], B("v4")[:, 1:4], T.even[:, 0:1], None, A.mult)
+        need("v", ub)
+        v_o3[h] = tt(B("o3")[:, 0:3], B("ua")[:, 0:3], B("ub")[:, 0:3], A.add)
+
+    def spread(h, queues):
+        for k in range(16):
+            a, b, q = k // 4, k % 4, queues[k % len(queues)]
+            need(q, v_o3[h])
+            Q[q].dma_start(T["ob%d" % h][32 * b:32 * b + 32, 3 * a:3 * a + 3], T["o3%d" % h][32 * a:32 * a + 32, 0:3]).then_inc(T.sem["lo%d" % h], 16)
+
+    def pick(h, qbuf, cbuf):
+        B, xg = T["ob%d" % h], T["xg%d" % h]
+        off = [T["%s%d" % (n, h)] for n in ("oa", "obb", "occ", "odd4")]
+        need("v", ("lo%d" % h, 256))
+        ot = [ts(off[k][:], B[:], float(k), None, A.add) for k in range(4)]
+        gat = lambda k: (xg[:, k:4 * W4:4], T.xs[:, 0:1024].indirect(off[k][:, 0:12]))
+        need("s", DX)
+        for k in (0, 1):
+            need("s", ot[k])
+            s_g = s(S.activation(*gat(k), F.Copy))
+        for k in (2, 3):
+            need("v", ot[k])
+            v_g = v(V.tensor_copy(*gat(k)))
+        need("v", s_g, v_g)
+        return v(V.quantize_mx(qbuf, cbuf, xg[:, 0:4 * W4]))
+
+    ls = [0]
+
+    def send(dsts, src, scol, dst, dcol, eng, sem):
+        for z in ("q", "c"):
+            tr = []
+            for k, d in enumerate(dsts):
+                rid, pid, _ = topo.addr(T.cores[d])
+                a, b = scol + CK * k, dcol(d)
+                sa, da = T[src + z][:, a:a + CK], T[dst + z][:, b:b + CK]
+                if z == "q":
+                    sa, da = sa.bitcast(dt.uint8), da.bitcast(dt.uint8)
+                tr.append(RemoteDMATransfer(dst_ids=[DstId(rid=rid, pnc=pid)], dma_engine_mask=(1 << eng[2 * k]) | (1 << eng[2 * k + 1]),
+                                            remote_sem=T.sem[sem], src=sa, dst=da))
+                ls[0] += 2
+            g.remote_dma_fused(tr, local_sem=T.sem.ls)
+
+    in_far = lambda d: CK * far_of(d).index(rank)
+    in_near = lambda d: CK * near_of(d).index(rank)
+
+    count(0)
+    invert(0)
+    spread(0, ["y"])
+    v_wn[1] = v(V.memset(T.wn1[:], 0.0))
+    count(1)
+    v_f = pick(0, T.tq[:, 0:W4], T.tc[:, 0:W4])
+    need("p", v_f)
+    send(far, "t", 0, "r", in_far, far_e, "af")
+    invert(1)
+    spread(1, ["y", "s"])
+    need("v", DW)
+    v_wq = v(V.quantize_mx(T.wq[:, 0:512], T.wc[:, 0:512], T.w1s[:, 0:2048]))
+    need("v", p_eb)
+    v_ebq = v(V.quantize_mx(T.eq[:, 0:512], T.ec[:, 0:512], T.eb[:, 0:2048]))
+    ts(T.icol[:, 0:1], T.p3[:, 0:1], 1.0, None, A.mult)
+    for k in range(4):
+        v_mk = ts(T.mk[:, k:k + 1], T.qi[:, 0:1], float(k), None, A.is_equal)
+    v(V.memset(T.pb[:, 0:16], 0.0))
+    v_last = v(V.memset(T.pl[:, 384:640], 0.0))
+    v_n = pick(1, T.nq[:, 0:W4], T["nc"][:, 0:W4])
+    need("p", v_n)
+    send(others, "n", 0, "n", lambda d: W4 + in_near(d), near_e, "an")
+
+    for h in range(2):
+        for m in range(3):
+            v_ol = ts(T["ol%d" % h][:, m:16:4], T["ob%d" % h][:, m:12:3], 0.25, None, A.mult)
+    need("v", v_ol, v_last, p_id)
+    for e in range(N):
+        h, a = where[e]
+        at = T.pl[:, 384:640].indirect(T["ol%d" % h][:, 4 * a:4 * a + 3])
+        x = v(V.tensor_copy(T.pl[:, CK * e:CK * e + CK], at))
+        need("v", x)
+        v_pl = v(V.tensor_copy(at, T.idr[:, CK * e:CK * e + CK]))
+        need("v", v_pl)
+
+    def expert(banks, xqv, xcv, ready, hb, qv, cv):
+        need("t", v_wq, *ready)
+        tm = [t(PE.matmul_mx(T["ps%d" % k][:, 0:W4], T.wq[:, 128 * i:128 * i + 128], T.wc[:, 128 * i:128 * i + 128], xqv, xcv, True, True)) for i, k in enumerate(banks)]
+        for i in (0, 2):
+            need("s", tm[i])
+            s_r = s(S.activation(hb[:, i:4 * W4:4], T["ps%d" % banks[i]][:, 0:W4], F.Relu, scale=0.05))
+            need("v", tm[i + 1])
+            v_r = ts(hb[:, i + 1:4 * W4:4], T["ps%d" % banks[i + 1]][:, 0:W4], 0.0, 0.05, A.max, A.mult)
+        need("v", s_r, v_r)
+        return v(V.quantize_mx(qv, cv, hb[:, 0:4 * W4])), [s_r, v_r]
+
+    v_hf, free_f = expert([0, 1, 2, 3], T.rq[:, 0:W4], T.rc[:, 0:W4], [("af", 16)], T.hf, T.hq[:, 0:W4], T.hc[:, 0:W4])
+    need("p", v_hf)
+    send(far, "h", 0, "d", in_far, far_e, "rf")
+    v_hn, free_n = expert([4, 5, 6, 7], T.nq[:, 144:336], T["nc"][:, 144:336], [("an", 12), v_n, v_svread[1], s_cnt[1]], T.hn, T.mq[:, 144:336], T.mc[:, 144:336])
+    need("p", v_hn)
+    send(others, "m", 192, "m", in_near, near_e, "rn")
+
+    need("s", v_pl, v_mk)
+    dg = [T["dg%d" % k] for k in range(4)]
+    for k in range(4):
+        s_dg = s(S.activation(dg[k][:], T.pl[:, k:640:4], F.Identity, scale=T.mk[:, k:k + 1]))
+    need("v", s_dg)
+    tt(T.d01[:], dg[0][:], dg[1][:], A.add)
+    need("v", tt(T.d23[:], dg[2][:], dg[3][:], A.add))
+    need("v", tt(T.dd[:], T.d01[:], T.d23[:], A.add))
+    v_op = ts(T.op[:], T.dd[:], T.icol[:, 0:1], None, A.add)
+
+    def unpack(c, banks, qv, cv, ready):
+        need("t", v_ebq, *ready)
+        tm = [t(PE.matmul_mx(T["ps%d" % k][:, 0:W4], T.eq[:, 128 * b:128 * b + 128], T.ec[:, 128 * b:128 * b + 128], qv, cv, True, True)) for b, k in enumerate(banks)]
+        base, end = 4 * W4 * c, 4 * W4 * c + 4 * W4
+        for b in (0, 2):
+            need("s", tm[b])
+            s_r = s(S.activation(T.dsb[:, base + b:end:4], T["ps%d" % banks[b]][:, 0:W4], F.Copy))
+            need("v", tm[b + 1])
+            v_r = v(V.tensor_copy(T.dsb[:, base + b + 1:end:4], T["ps%d" % banks[b + 1]][:, 0:W4]))
+        return [s_r, v_r]
+
+    for c in sorted(range(2), key=lambda h: min(X[h])):
+        if c == 0:
+            ready = unpack(0, [0, 1, 2, 3], T.dq[:, 0:W4], T.dc[:, 0:W4], [("rf", 16)] + free_f)
+        else:
+            ready = unpack(1, [4, 5, 6, 7], T.mq[:, 0:W4], T.mc[:, 0:W4], [("rn", 12), v_hn] + free_n)
+        need("v", v_op, *ready)
+        for e in sorted(X[c]):
+            d, o = 4 * W4 * c + W4 * where[e][1], 16 + W4 * e
+            x = tt(T.pb[:, o:o + W4], T.pb[:, 0:o].indirect(T.op[:, 12 * e:12 * e + 12]), T.dsb[:, d:d + W4], A.add)
+            need("v", x)
+    win = T.pb[:, 0:16 + N * W4]
+    need("s", x)
+    s_y = s(S.activation(T.yt[:, 512:1024], win.indirect(T.op[:, 128:160]), F.Copy))
+    v_y = v(V.tensor_copy(T.yt[:, 0:512], win.indirect(T.op[:, 96:128])))
+    need("y", v_y)
+    g.sync.dma_start(T.y[:, 0:512], T.yt[:, 0:512]).then_inc(T.sem.dy, 16)
+    need("s", s_y)
+    g.scalar.dma_start(T.y[:, 512:1024], T.yt[:, 512:1024]).then_inc(T.sem.dy, 16)
+
+    need("p", ("ls", ls[0]), ("dwg", 16), DX, DW, ("lo0", 256), ("lo1", 256), ("af", 16), ("an", 12), ("rf", 16), ("rn", 12), ("dy", 32))
+    need("p", *[(q, cnt[q]) for q in ("v", "s", "t", "p")])

@@ -3,9 +3,9 @@ from concourse.mybir import dt, AluOpType as A, ActivationFunctionType as F
 
 CK = 48
 W4 = 4 * CK
-VB = [0, 1, 2, 3, 4]
-SB = [5, 6, 7]
-NV = len(VB)
+VB = [0, 1, 2, 3]
+SB = [4, 5, 6, 7]
+NV, NS = len(VB), len(SB)
 
 SCRATCH = {}
 
@@ -17,14 +17,14 @@ def _sbuf(dtype, names):
             SCRATCH[m] = ("sbuf", [128, int(c)], dtype)
 
 
-_sbuf("bfloat16", "wgs:32 xs:1024 w1s:2048 onesb:2048 eb:2048 d0blk:256 d0cnt:%d hf:768 hn:768 gt@:512 cmp@:%d cs@:%d sg@:%d eqb@:256 es@:256 xg@:768"
-      % (256 * NV, 256 * NV, 256 * NV, 256 * len(SB)))
+_sbuf("bfloat16", "wgs:32 xs:1024 xp:1024 w1s:2048 ones:516 z:516 d0blk:256 d0cnt:%d hh:1536 gt@:512 cmp@:%d cs@:%d sg@:%d eqb@:256 es@:256 xg@:768"
+      % (256 * NV, 256 * NV, 256 * NV, 256 * NS))
 for _d, _s in (("float8_e4m3fn_x4", "q"), ("uint8", "c")):
-    _sbuf(_d, " ".join("%s%s%s" % (w[0], _s, w[1:]) for w in "x:256 w:512 e:512 t:192 r:192 n:336 h:192 d:192 m:336 g@:128".split()))
-_sbuf("int32", "ic:32 p3:32 ib:256 ibm:256 hi:8 qi:8")
-_sbuf("float32", "odd:4 even:4 h64:4 icol:4 mk:4 tok0:128 tokv:128 idr:384 pl:640 dg0:160 dg1:160 dg2:160 dg3:160 d01:160 d23:160 dd:160 dsb:1536 pb:1552 yt:1024")
-_sbuf("float32", "tt@:256 ac@:8 a2@:4 a3@:4 rk@:8 wn@:272 t2@:128 v4@:4 ua@:4 ub@:4 o3@:4 ob@:12")
-_sbuf("uint16", "op:160 go@:32 ru@:8 ol@:16 oa@:12 obb@:12 occ@:12 odd4@:12")
+    _sbuf(_d, " ".join("%s%s%s" % (w[0], _s, w[1:]) for w in "x:256 w:512 e:512 t:192 n:528 m:720 g@:128".split()))
+_sbuf("int32", "ic:1 p3:1 h16i:1 q12:1 ib:256 ibm:256")
+_sbuf("float32", "e4:64 p3f:1 h16:1 mk:4 tok0:128 tokv:128 idr:384 pl:640 dg0:160 dg1:160 dg2:160 dg3:160 d01:160 d23:160 dd:160")
+_sbuf("float32", "ds@:768 pb:%d yt:1024 tt@:256 ac@:8 a2@:4 a3@:4 rk@:8 wn@:256 la@:12 lb@:12 ob@:12" % (16 + 8 * W4))
+_sbuf("uint16", "go:64 op:160 ru@:8 ol@:16 of@:12")
 for _b in range(8):
     SCRATCH["ps%d" % _b] = ("psum", [128, 512], "float32")
 
@@ -39,7 +39,8 @@ def rank_program(g, core, T, topo):
     near_of = lambda r: [k for k in range(N) if k != r and topo.chip(T.cores[k]) == topo.chip(T.cores[r])]
     far_of = lambda r: [k for k in range(N) if topo.chip(T.cores[k]) != topo.chip(T.cores[r])]
     others, far = near_of(rank), far_of(rank)
-    X = [far, others + [rank]]
+    kind = ["far", "near"] if 0 in far else ["near", "far"]
+    X = [{"far": far, "near": others + [rank]}[k] for k in kind]
     where = {e: (h, a) for h in range(2) for a, e in enumerate(X[h])}
     far_e = topo.engines(core, T.cores[far[0]])
     near_e = [e for e in topo.engines(core, T.cores[others[0]]) if e not in far_e]
@@ -68,63 +69,59 @@ def rank_program(g, core, T, topo):
     tt = lambda out, a, b, op: v(V.tensor_tensor(out, a, b, op))
 
     g.sync.dma_start(T.wgs[:], T.wg[:, 0:32]).then_inc(T.sem.dwg, 16)
-    g.sync.dma_start(T.xs[:, 0:512], T.x[:, 0:512]).then_inc(T.sem.dx, 16)
     g.scalar.dma_start(T.xs[:, 512:1024], T.x[:, 512:1024]).then_inc(T.sem.dx, 16)
+    g.sync.dma_start(T.xs[:, 0:512], T.x[:, 0:512]).then_inc(T.sem.dx, 16)
     g.sync.dma_start(T.w1s[:], T.w1[:]).then_inc(T.sem.dw, 16)
     DWG, DX, DW = ("dwg", 16), ("dx", 32), ("dw", 16)
 
-    p_ic = p(g.iota(T.ic[:], [[0, 32]], 0, 1))
+    imp = dict(allow_small_or_imprecise_dtypes=True)
+    p_ic = p(g.iota(T.ic[:], [[0, 1]], 0, 1))
+    for k, e in enumerate(X[0] + X[1]):
+        p_e4 = p(g.iota(T.e4[:, 8 * k:8 * k + 8], [[0, 8]], 4 * e, 0, **imp))
+    p_tok = p(g.iota(T.tok0[:], [[32, 8], [1, 16]], 0, 0, **imp))
     p_ib = p(g.iota(T.ib[:], [[1, 256]], 128, -1))
-    p_tok = p(g.iota(T.tok0[:], [[128, 8], [4, 16]], 0, 0, allow_small_or_imprecise_dtypes=True))
-    v_ones = v(V.memset(T.onesb[:], 1.0))
+    v_ones = v(V.memset(T.ones[:], 1.0))
     need("p", v_ones)
-    p_eb = p(g.affine_select(T.eb[:], T.onesb[:], [[1, 4], [-1, 512]], A.is_equal, 0.0, 0, 4))
-    p_id = p(g.iota(T.idr[:], [[W4, N], [4, CK]], 16, 0, allow_small_or_imprecise_dtypes=True))
+    p_z = p(g.affine_select(T.z[:], T.ones[:], [[-1, 516]], A.is_equal, 0.0, 3, 4))
+    p_id = p(g.iota(T.idr[:], [[W4, N], [4, CK]], 16, 0, **imp))
+
     need("v", p_ic)
     v_p3 = ts(T.p3[:], T.ic[:], 3, None, A.bitwise_and)
-    v_hi = ts(T.hi[:, 0:1], T.ic[:, 0:1], 4, 1, A.logical_shift_right, A.bitwise_and)
-    v_qi = ts(T.qi[:, 0:1], T.ic[:, 0:1], 2, 3, A.logical_shift_right, A.bitwise_and)
+    v_h16i = ts(T.h16i[:], T.ic[:], 16, None, A.bitwise_and)
+    v_q12 = ts(T.q12[:], T.ic[:], 12, None, A.bitwise_and)
     need("v", v_p3)
-    v_go = [None, None]
-    for h in range(2):
-        for a in range(4):
-            v_go[h] = ts(T["go%d" % h][:, 8 * a:8 * a + 8], T.p3[:, 8 * a:8 * a + 8], 4 * X[h][a], None, A.add)
-    s_gt = [None, None]
-    need("s", DWG)
-    for h in range(2):
-        need("s", v_go[h])
-        s_gt[h] = s(S.activation(T["gt%d" % h][:], T.wgs[:, 0:32].indirect(T["go%d" % h][:, 0:32]), F.Copy))
+    v_p3f = ts(T.p3f[:], T.p3[:], 1.0, None, A.mult)
+    need("v", v_h16i)
+    v_h16 = ts(T.h16[:], T.h16i[:], 1.0, None, A.mult)
+    need("v", v_p3f, p_e4)
+    v_go = ts(T.go[:], T.e4[:], T.p3f[:, 0:1], None, A.add)
     v_d1 = v(V.memset(T.d0cnt[:], 1.0))
-    need("v", v_hi, v_qi)
-    v_odd = ts(T.odd[:, 0:1], T.hi[:, 0:1], 1.0, None, A.mult)
-    v_h64 = ts(T.h64[:, 0:1], T.hi[:, 0:1], 64.0, None, A.mult)
-    v_even = ts(T.even[:, 0:1], T.hi[:, 0:1], -1.0, 1.0, A.mult, A.add)
-    need("v", p_ib)
-    v_ibm = ts(T.ibm[:], T.ib[:], 31, None, A.bitwise_and)
-    need("v", v_d1)
-    v_d0 = v(V.memset(T.d0cnt[:, 0:256 * NV:256], 0.0))
-    v_z = [v(V.memset(T["ac%d" % h][:], 0.0)) for h in range(2)]
-    need("v", v_h64, p_tok)
-    v_tok = ts(T.tokv[:], T.tok0[:], T.h64[:, 0:1], None, A.add)
-    v_wn = [v(V.memset(T.wn0[:], 0.0)), None]
-    need("v", v_ibm)
-    v_blk = ts(T.d0blk[:], T.ibm[:], 0, None, A.not_equal)
+    need("v", DWG, v_go)
+    v_gt = v(V.tensor_copy(T.gt0[:, 0:256], T.wgs[:, 0:32].indirect(T.go[:, 0:16])))
+    need("s", DWG, v_go)
+    s_gt0 = s(S.activation(T.gt0[:, 256:512], T.wgs[:, 0:32].indirect(T.go[:, 16:32]), F.Copy))
+    s_gt1 = s(S.activation(T.gt1[:], T.wgs[:, 0:32].indirect(T.go[:, 32:64]), F.Copy))
+    need("v", v_gt, s_gt0)
+    v_gq = [v(V.quantize_mx(T.gq0[:, 0:128], T.gc0[:, 0:128], T.gt0[:, 0:512])), None]
 
-    need("v", s_gt[0])
-    v_gq0 = v(V.quantize_mx(T.gq0[:, 0:128], T.gc0[:, 0:128], T.gt0[:, 0:512]))
     need("v", DX)
     v_xq = v(V.quantize_mx(T.xq[:, 0:256], T.xc[:, 0:256], T.xs[:, 0:1024]))
-    need("v", s_gt[1])
-    v_gq1 = v(V.quantize_mx(T.gq1[:, 0:128], T.gc1[:, 0:128], T.gt1[:, 0:512]))
+    v_z = [v(V.memset(T["ac%d" % h][:, 7:8], 0.0)) for h in range(2)]
+    plane = lambda k: (T.xp[:, 256 * k:256 * k + 256], T.xs[:, k:1024:4])
+    v_xp = v(V.tensor_copy(*plane(3)))
+    need("s", DX)
+    s(S.activation(*plane(0), F.Copy))
     sv, ss = [T.ps4, T.ps6], [T.ps5, T.ps7]
     t_sv, t_ss = [None, None], [None, None]
-    for h in range(2):
-        need("t", v_xq, (v_gq0, v_gq1)[h])
+
+    def score(h):
+        need("t", v_xq, v_gq[h])
         mm = lambda out: t(PE.matmul_mx(out, T["gq%d" % h][:, 0:128], T["gc%d" % h][:, 0:128], T.xq[:, 0:256], T.xc[:, 0:256], True, True))
         t_sv[h] = mm(sv[h][:, 0:256])
         t_ss[h] = mm(ss[h][:, 0:256])
 
     s_cnt, v_cnt, v_es, v_svread = [None, None], [None, None], [None, None], [None, None]
+    const = {}
 
     def count(h):
         P, own, cm, PS, sg, ac = sv[h], T["tt%d" % h], T["cmp%d" % h], ss[h], T["sg%d" % h], T["ac%d" % h]
@@ -135,80 +132,80 @@ def rank_program(g, core, T, topo):
         for u, b in enumerate(SB):
             need("s", sgn[u])
             m = 256 * u + 32 * (b + 1)
-            lo, hi = sg[:, 256 * u:m], sg[:, m:256 * u + 256]
+            lo = sg[:, 256 * u:m]
             s_cnt[h] = s(S.activation(lo, lo, F.Sign, bias=1.0, scale=-2.0, accum_out=ac[:, u:u + 1]))
             if b < 7:
-                s_cnt[h] = s(S.activation(hi, hi, F.Sign, bias=-1.0, scale=-2.0, accum_out=ac[:, 3 + u:4 + u]))
+                hi = sg[:, m:256 * u + 256]
+                s_cnt[h] = s(S.activation(hi, hi, F.Sign, bias=-1.0, scale=-2.0, accum_out=ac[:, NS + u:NS + u + 1]))
         need("v", v_tt)
         v_eq = tt(T["eqb%d" % h][:], P[:, 0:256], own[:], A.is_equal)
         for u, b in enumerate(VB):
             m = 32 * (b + 1)
             ts(cm[:, 256 * u:256 * u + m], P[:, 0:m], own[:, 32 * b:32 * b + 1], None, A.is_ge)
             v_svread[h] = ts(cm[:, 256 * u + m:256 * u + 256], P[:, m:256], own[:, 32 * b:32 * b + 1], None, A.is_gt)
-        need("v", v_eq, v_blk)
-        v_es[h] = v(V.tensor_tensor_scan(T["es%d" % h][:], T.d0blk[:], T["eqb%d" % h][:], 0.0, A.mult, A.add))
-        need("v", v_svread[h], v_d0)
+        if h == 0:
+            need("v", v_d1, p_ib)
+            v_ibm = ts(T.ibm[:], T.ib[:], 31, None, A.bitwise_and)
+            const["d0"] = v(V.memset(T.d0cnt[:, 0:256 * NV:256], 0.0))
+            need("v", v_ibm)
+            const["blk"] = ts(T.d0blk[:], T.ibm[:], 0, None, A.not_equal)
+            need("v", s_gt1)
+            v_gq[1] = v(V.quantize_mx(T.gq1[:, 0:128], T.gc1[:, 0:128], T.gt1[:, 0:512]))
+        need("v", v_svread[h], const["d0"])
         v_cnt[h] = v(V.tensor_tensor_scan(T["cs%d" % h][:], T.d0cnt[:], cm[:], 0.0, A.mult, A.add))
+        need("v", v_eq, const["blk"])
+        v_es[h] = v(V.tensor_tensor_scan(T["es%d" % h][:], T.d0blk[:], T["eqb%d" % h][:], 0.0, A.mult, A.add))
+        if h == 0:
+            need("v", p_tok, v_h16)
+            const["tok"] = ts(T.tokv[:], T.tok0[:], T.h16[:, 0:1], None, A.add)
+            const["wn"] = [v(V.memset(T["wn%d" % k][:, 0:CK], 0.0)) for k in range(2)]
 
-    v_o3 = [None, None]
-
-    def invert(h):
+    def invert(h, queues):
         B = lambda n: T["%s%d" % (n, h)]
-        need("v", s_cnt[h])
-        x2 = tt(B("a2")[:, 0:3], B("ac")[:, 0:3], B("ac")[:, 3:6], A.add)
         need("v", v_cnt[h], v_es[h])
         tt(B("rk")[:, 0:NV], B("cs")[:, 255:256 * NV:256], B("es")[:, 31:32 * NV:32], A.subtract)
+        need("v", s_cnt[h])
+        x2 = tt(B("a2")[:, 0:NS], B("ac")[:, 0:NS], B("ac")[:, NS:2 * NS], A.add)
         need("v", x2)
-        x3 = ts(B("a3")[:, 0:3], B("a2")[:, 0:3], 0.5, 128.0, A.mult, A.add)
+        x3 = ts(B("a3")[:, 0:NS], B("a2")[:, 0:NS], 0.5, 128.0, A.mult, A.add)
         need("v", x3)
-        r2 = tt(B("rk")[:, NV:8], B("a3")[:, 0:3], B("es")[:, 32 * NV + 31:256:32], A.subtract)
+        r2 = tt(B("rk")[:, NV:8], B("a3")[:, 0:NS], B("es")[:, 32 * NV + 31:256:32], A.subtract)
         need("v", r2)
-        ru = ts(B("ru")[:, 0:8], B("rk")[:, 0:8], 16.0, None, A.add)
-        need("v", ru, v_tok, v_wn[h])
-        w = v(V.tensor_copy(B("wn")[:, 0:272].indirect(B("ru")[:, 0:8]), T.tokv[:, 0:128]))
-        need("v", w)
-        ta = v(V.transpose(B("t2")[:, 0:64], B("wn")[:, 0:64]))
-        tb = v(V.transpose(B("t2")[:, 64:128], B("wn")[:, 16:80]))
-        need("v", ta)
-        tt(B("v4")[:, 0:4:2], B("t2")[:, 0:64:32], B("t2")[:, 16:64:32], A.add)
-        need("v", tb)
-        vb = tt(B("v4")[:, 1:4:2], B("t2")[:, 64:128:32], B("t2")[:, 80:128:32], A.add)
-        need("v", vb, v_odd, v_even)
-        ts(B("ua")[:, 0:3], B("v4")[:, 0:3], T.odd[:, 0:1], None, A.mult)
-        ub = ts(B("ub")[:, 0:3], B("v4")[:, 1:4], T.even[:, 0:1], None, A.mult)
-        need("v", ub)
-        v_o3[h] = tt(B("o3")[:, 0:3], B("ua")[:, 0:3], B("ub")[:, 0:3], A.add)
+        ru = ts(B("ru")[:, 0:8], B("rk")[:, 0:8], 1.0, None, A.mult)
+        need("v", ru, const["tok"], const["wn"][h])
+        w = v(V.tensor_copy(B("wn")[:, 0:256].indirect(B("ru")[:, 0:8]), T.tokv[:, 0:128]))
+        for k in range(8):
+            a, half, q = k // 2, k % 2, queues[k % len(queues)]
+            need(q, w)
+            lst = B("wn")[32 * a + 16 * half:32 * a + 16 * half + 8, 0:CK]
+            Q[q].dma_start(B("lb" if half else "la")[:, 3 * a:3 * a + 3], lst).then_inc(T.sem["lo%d" % h], 16)
 
-    def spread(h, queues):
-        for k in range(16):
-            a, b, q = k // 4, k % 4, queues[k % len(queues)]
-            need(q, v_o3[h])
-            Q[q].dma_start(T["ob%d" % h][32 * b:32 * b + 32, 3 * a:3 * a + 3], T["o3%d" % h][32 * a:32 * a + 32, 0:3]).then_inc(T.sem["lo%d" % h], 16)
+    v_of, v_ob = [None, None], [None, None]
 
     def pick(h, qbuf, cbuf):
-        B, xg = T["ob%d" % h], T["xg%d" % h]
-        off = [T["%s%d" % (n, h)] for n in ("oa", "obb", "occ", "odd4")]
-        need("v", ("lo%d" % h, 256))
-        ot = [ts(off[k][:], B[:], float(k), None, A.add) for k in range(4)]
-        gat = lambda k: (xg[:, k:4 * W4:4], T.xs[:, 0:1024].indirect(off[k][:, 0:12]))
-        need("s", DX)
+        xg, of = T["xg%d" % h], T["of%d" % h]
+        need("v", ("lo%d" % h, 128))
+        v_ob[h] = tt(T["ob%d" % h][:], T["la%d" % h][:], T["lb%d" % h][:], A.add)
+        need("v", v_ob[h])
+        v_of[h] = ts(of[:], T["ob%d" % h][:], 1.0, None, A.mult)
+        gat = lambda k: (xg[:, k:4 * W4:4], T.xp[:, 256 * k:256 * k + 256].indirect(of[:, 0:12]))
+        need("s", s_xp, v_xp, v_of[h])
+        need("v", s_xp, v_xp, v_of[h])
         for k in (0, 1):
-            need("s", ot[k])
             s_g = s(S.activation(*gat(k), F.Copy))
         for k in (2, 3):
-            need("v", ot[k])
             v_g = v(V.tensor_copy(*gat(k)))
         need("v", s_g, v_g)
         return v(V.quantize_mx(qbuf, cbuf, xg[:, 0:4 * W4]))
 
     ls = [0]
 
-    def send(dsts, src, scol, dst, dcol, eng, sem):
+    def send(parts):
         for z in ("q", "c"):
             tr = []
-            for k, d in enumerate(dsts):
+            for d, src, a, dst, b, sem in parts:
                 rid, pid, _ = topo.addr(T.cores[d])
-                a, b = scol + CK * k, dcol(d)
+                k, eng = (far.index(d), far_e) if d in far else (others.index(d), near_e)
                 sa, da = T[src + z][:, a:a + CK], T[dst + z][:, b:b + CK]
                 if z == "q":
                     sa, da = sa.bitcast(dt.uint8), da.bitcast(dt.uint8)
@@ -220,89 +217,121 @@ def rank_program(g, core, T, topo):
     in_far = lambda d: CK * far_of(d).index(rank)
     in_near = lambda d: CK * near_of(d).index(rank)
 
+    def dispatch(h):
+        src = "t" if kind[h] == "far" else "n"
+        x = pick(h, T[src + "q"][:, 0:W4], T[src + "c"][:, 0:W4])
+        need("p", x)
+        if kind[h] == "far":
+            send([(d, "t", CK * k, "n", 336 + in_far(d), "af") for k, d in enumerate(far)])
+        else:
+            send([(d, "n", CK * k, "n", W4 + in_near(d), "an") for k, d in enumerate(others)])
+        return x
+
+    table = T.pl[:, 384:640]
+    v_chain = [None, None]
+
+    def chain(h):
+        need("v", v_ob[h])
+        for m in range(3):
+            x = ts(T["ol%d" % h][:, m:16:4], T["ob%d" % h][:, m:12:3], 1.0, None, A.mult)
+        need("v", x, v_fresh, p_id)
+        for e in sorted(X[h]):
+            a = where[e][1]
+            at = table.indirect(T["ol%d" % h][:, 4 * a:4 * a + 3])
+            o = W4 * h + CK * a
+            if e == 0:
+                x = v(V.memset(T.pl[:, o:o + CK], 0.0))
+            else:
+                x = v(V.tensor_copy(T.pl[:, o:o + CK], at))
+            need("v", x)
+            x = v(V.tensor_copy(at, T.idr[:, CK * e:CK * e + CK]))
+            need("v", x)
+        v_chain[h] = x
+
+    score(0)
     count(0)
-    invert(0)
-    spread(0, ["y"])
-    v_wn[1] = v(V.memset(T.wn1[:], 0.0))
+    score(1)
+    for k in (1, 2):
+        s_xp = s(S.activation(*plane(k), F.Copy))
+    invert(0, ["y"])
     count(1)
-    v_f = pick(0, T.tq[:, 0:W4], T.tc[:, 0:W4])
-    need("p", v_f)
-    send(far, "t", 0, "r", in_far, far_e, "af")
-    invert(1)
-    spread(1, ["y", "s"])
+    invert(1, ["y", "s"])
+    v_x = [dispatch(0), None]
     need("v", DW)
     v_wq = v(V.quantize_mx(T.wq[:, 0:512], T.wc[:, 0:512], T.w1s[:, 0:2048]))
-    need("v", p_eb)
-    v_ebq = v(V.quantize_mx(T.eq[:, 0:512], T.ec[:, 0:512], T.eb[:, 0:2048]))
-    ts(T.icol[:, 0:1], T.p3[:, 0:1], 1.0, None, A.mult)
-    for k in range(4):
-        v_mk = ts(T.mk[:, k:k + 1], T.qi[:, 0:1], float(k), None, A.is_equal)
-    v(V.memset(T.pb[:, 0:16], 0.0))
-    v_last = v(V.memset(T.pl[:, 384:640], 0.0))
-    v_n = pick(1, T.nq[:, 0:W4], T["nc"][:, 0:W4])
-    need("p", v_n)
-    send(others, "n", 0, "n", lambda d: W4 + in_near(d), near_e, "an")
+    v_fresh = v(V.memset(table, 0.0))
+    v_x[1] = dispatch(1)
+    chain(0)
+    chain(1)
+    need("v", p_z)
+    for b in range(4):
+        v_ebq = v(V.quantize_mx(T.eq[:, 128 * b:128 * b + 128], T.ec[:, 128 * b:128 * b + 128], T.z[:, 3 - b:515 - b]))
 
-    for h in range(2):
-        for m in range(3):
-            v_ol = ts(T["ol%d" % h][:, m:16:4], T["ob%d" % h][:, m:12:3], 0.25, None, A.mult)
-    need("v", v_ol, v_last, p_id)
-    for e in range(N):
-        h, a = where[e]
-        at = T.pl[:, 384:640].indirect(T["ol%d" % h][:, 4 * a:4 * a + 3])
-        x = v(V.tensor_copy(T.pl[:, CK * e:CK * e + CK], at))
-        need("v", x)
-        v_pl = v(V.tensor_copy(at, T.idr[:, CK * e:CK * e + CK]))
-        need("v", v_pl)
+    def addresses():
+        need("v", v_q12)
+        for k in range(4):
+            v_mk = ts(T.mk[:, k:k + 1], T.q12[:], float(4 * k), None, A.is_equal)
+        v(V.memset(T.pb[:, 0:16], 0.0))
+        need("s", v_chain[1], v_mk)
+        dg = [T["dg%d" % k] for k in range(4)]
+        for k in range(4):
+            s_dg = s(S.activation(dg[k][:], T.pl[:, k:640:4], F.Identity, scale=T.mk[:, k:k + 1]))
+        need("v", s_dg)
+        tt(T.d01[:], dg[0][:], dg[1][:], A.add)
+        need("v", tt(T.d23[:], dg[2][:], dg[3][:], A.add))
+        need("v", tt(T.dd[:], T.d01[:], T.d23[:], A.add))
+        return ts(T.op[:], T.dd[:], T.p3f[:, 0:1], None, A.add)
 
-    def expert(banks, xqv, xcv, ready, hb, qv, cv):
-        need("t", v_wq, *ready)
-        tm = [t(PE.matmul_mx(T["ps%d" % k][:, 0:W4], T.wq[:, 128 * i:128 * i + 128], T.wc[:, 128 * i:128 * i + 128], xqv, xcv, True, True)) for i, k in enumerate(banks)]
+    def expert():
+        need("t", v_wq, v_x[kind.index("near")], ("an", 12), ("af", 16))
+        W8 = 2 * W4
+        tm = [t(PE.matmul_mx(T["ps%d" % i][:, 0:W8], T.wq[:, 128 * i:128 * i + 128], T.wc[:, 128 * i:128 * i + 128],
+                             T.nq[:, 144:528], T["nc"][:, 144:528], True, True)) for i in range(4)]
         for i in (0, 2):
             need("s", tm[i])
-            s_r = s(S.activation(hb[:, i:4 * W4:4], T["ps%d" % banks[i]][:, 0:W4], F.Relu, scale=0.05))
+            s_r = s(S.activation(T.hh[:, i:4 * W8:4], T["ps%d" % i][:, 0:W8], F.Relu, scale=0.05))
             need("v", tm[i + 1])
-            v_r = ts(hb[:, i + 1:4 * W4:4], T["ps%d" % banks[i + 1]][:, 0:W4], 0.0, 0.05, A.max, A.mult)
+            v_r = ts(T.hh[:, i + 1:4 * W8:4], T["ps%d" % (i + 1)][:, 0:W8], 0.0, 0.05, A.max, A.mult)
         need("v", s_r, v_r)
-        return v(V.quantize_mx(qv, cv, hb[:, 0:4 * W4])), [s_r, v_r]
+        x = v(V.quantize_mx(T.mq[:, 144:528], T.mc[:, 144:528], T.hh[:, 0:4 * W8]))
+        need("p", x)
+        send([(d, "m", 336 + CK * k, "m", 528 + in_far(d), "rf") for k, d in enumerate(far)]
+             + [(d, "m", W4 + CK * k, "m", in_near(d), "rn") for k, d in enumerate(others)])
+        return x, [s_r, v_r]
 
-    v_hf, free_f = expert([0, 1, 2, 3], T.rq[:, 0:W4], T.rc[:, 0:W4], [("af", 16)], T.hf, T.hq[:, 0:W4], T.hc[:, 0:W4])
-    need("p", v_hf)
-    send(far, "h", 0, "d", in_far, far_e, "rf")
-    v_hn, free_n = expert([4, 5, 6, 7], T.nq[:, 144:336], T["nc"][:, 144:336], [("an", 12), v_n, v_svread[1], s_cnt[1]], T.hn, T.mq[:, 144:336], T.mc[:, 144:336])
-    need("p", v_hn)
-    send(others, "m", 192, "m", in_near, near_e, "rn")
+    v_h, free = expert()
+    v_op = addresses()
 
-    need("s", v_pl, v_mk)
-    dg = [T["dg%d" % k] for k in range(4)]
-    for k in range(4):
-        s_dg = s(S.activation(dg[k][:], T.pl[:, k:640:4], F.Identity, scale=T.mk[:, k:k + 1]))
-    need("v", s_dg)
-    tt(T.d01[:], dg[0][:], dg[1][:], A.add)
-    need("v", tt(T.d23[:], dg[2][:], dg[3][:], A.add))
-    need("v", tt(T.dd[:], T.d01[:], T.d23[:], A.add))
-    v_op = ts(T.op[:], T.dd[:], T.icol[:, 0:1], None, A.add)
-
-    def unpack(c, banks, qv, cv, ready):
+    def unpack(pieces, banks, qv, cv, ready):
         need("t", v_ebq, *ready)
         tm = [t(PE.matmul_mx(T["ps%d" % k][:, 0:W4], T.eq[:, 128 * b:128 * b + 128], T.ec[:, 128 * b:128 * b + 128], qv, cv, True, True)) for b, k in enumerate(banks)]
-        base, end = 4 * W4 * c, 4 * W4 * c + 4 * W4
         for b in (0, 2):
-            need("s", tm[b])
-            s_r = s(S.activation(T.dsb[:, base + b:end:4], T["ps%d" % banks[b]][:, 0:W4], F.Copy))
-            need("v", tm[b + 1])
-            v_r = v(V.tensor_copy(T.dsb[:, base + b + 1:end:4], T["ps%d" % banks[b + 1]][:, 0:W4]))
+            for q, f in (("s", b), ("v", b + 1)):
+                need(q, tm[f])
+                for lo, hi, buf, at in pieces:
+                    o, i = buf[:, 4 * at + f:4 * (at + hi - lo):4], T["ps%d" % banks[f]][:, lo:hi]
+                    if q == "s":
+                        s_r = s(S.activation(o, i, F.Copy))
+                    else:
+                        v_r = v(V.tensor_copy(o, i))
         return [s_r, v_r]
 
-    for c in sorted(range(2), key=lambda h: min(X[h])):
+    for c in range(2):
+        ds = T["ds%d" % c]
+        pieces = [(0, W4, ds, 0)]
         if c == 0:
-            ready = unpack(0, [0, 1, 2, 3], T.dq[:, 0:W4], T.dc[:, 0:W4], [("rf", 16)] + free_f)
+            z = CK * where[0][1]
+            pieces = [(z, z + CK, T.pb, 4)] + [(lo, hi, ds, lo) for lo, hi in ((0, z), (z + CK, W4)) if lo < hi]
+        if kind[c] == "far":
+            ready = unpack(pieces, [0, 1, 2, 3], T.mq[:, 528:720], T.mc[:, 528:720], [("rf", 16)] + free)
         else:
-            ready = unpack(1, [4, 5, 6, 7], T.mq[:, 0:W4], T.mc[:, 0:W4], [("rn", 12), v_hn] + free_n)
+            ready = unpack(pieces, [4, 5, 6, 7], T.mq[:, 0:W4], T.mc[:, 0:W4], [("rn", 12), v_h, v_svread[1], s_cnt[1]])
         need("v", v_op, *ready)
         for e in sorted(X[c]):
-            d, o = 4 * W4 * c + W4 * where[e][1], 16 + W4 * e
-            x = tt(T.pb[:, o:o + W4], T.pb[:, 0:o].indirect(T.op[:, 12 * e:12 * e + 12]), T.dsb[:, d:d + W4], A.add)
+            if e == 0:
+                continue
+            d, o, k = W4 * where[e][1], 16 + W4 * e, 48 * c + 12 * where[e][1]
+            x = tt(T.pb[:, o:o + W4], T.pb[:, 0:o].indirect(T.op[:, k:k + 12]), ds[:, d:d + W4], A.add)
             need("v", x)
     win = T.pb[:, 0:16 + N * W4]
     need("s", x)
@@ -313,5 +342,5 @@ def rank_program(g, core, T, topo):
     need("s", s_y)
     g.scalar.dma_start(T.y[:, 512:1024], T.yt[:, 512:1024]).then_inc(T.sem.dy, 16)
 
-    need("p", ("ls", ls[0]), ("dwg", 16), DX, DW, ("lo0", 256), ("lo1", 256), ("af", 16), ("an", 12), ("rf", 16), ("rn", 12), ("dy", 32))
+    need("p", ("ls", ls[0]), ("dwg", 16), DX, DW, ("lo0", 128), ("lo1", 128), ("af", 16), ("an", 12), ("rf", 16), ("rn", 12), ("dy", 32))
     need("p", *[(q, cnt[q]) for q in ("v", "s", "t", "p")])

from concourse.bass import DstId, RemoteDMATransfer
from concourse.mybir import dt, AluOpType as A, ActivationFunctionType as F

CK = 48
W4 = 4 * CK
VB = [0, 1, 2, 3]
SB = [4, 5, 6, 7]
NV, NS = len(VB), len(SB)

SCRATCH = {}


def _sbuf(dtype, names):
    for w in names.split():
        n, c = w.split(":")
        for m in ([n[:-1] + "0", n[:-1] + "1"] if n.endswith("@") else [n]):
            SCRATCH[m] = ("sbuf", [128, int(c)], dtype)


_sbuf("bfloat16", "wgs:32 xs:1024 xp:1024 w1s:2048 ones:516 z:516 d0blk:256 d0cnt:%d hh:1536 gt@:512 cmp@:%d cs@:%d sg@:%d eqb@:256 es@:256 xg@:768"
      % (256 * NV, 256 * NV, 256 * NV, 256 * NS))
for _d, _s in (("float8_e4m3fn_x4", "q"), ("uint8", "c")):
    _sbuf(_d, " ".join("%s%s%s" % (w[0], _s, w[1:]) for w in "x:256 w:512 e:512 t:192 n:528 m:720 g@:128".split()))
_sbuf("int32", "ic:1 p3:1 h16i:1 q12:1 ib:256 ibm:256")
_sbuf("float32", "e4:64 p3f:1 h16:1 mk:4 tok0:128 tokv:128 idr:384 pl:640 dg0:160 dg1:160 dg2:160 dg3:160 d01:160 d23:160 dd:160")
_sbuf("float32", "ds@:768 pb:%d yt:1024 tt@:256 ac@:8 a2@:4 a3@:4 rk@:8 wn@:256 la@:12 lb@:12 ob@:12" % (16 + 8 * W4))
_sbuf("uint16", "go:64 op:160 ru@:8 ol@:16 of@:12")
for _b in range(8):
    SCRATCH["ps%d" % _b] = ("psum", [128, 512], "float32")

SEMAPHORES = ["v", "t", "s", "p", "dwg", "dx", "dw", "lo0", "lo1", "af", "an", "rf", "rn", "ls", "dy"]


def rank_program(g, core, T, topo):
    rank = T.rank_of(core)
    if rank is None:
        return
    N = len(T.cores)
    near_of = lambda r: [k for k in range(N) if k != r and topo.chip(T.cores[k]) == topo.chip(T.cores[r])]
    far_of = lambda r: [k for k in range(N) if topo.chip(T.cores[k]) != topo.chip(T.cores[r])]
    others, far = near_of(rank), far_of(rank)
    kind = ["far", "near"] if 0 in far else ["near", "far"]
    X = [{"far": far, "near": others + [rank]}[k] for k in kind]
    where = {e: (h, a) for h in range(2) for a, e in enumerate(X[h])}
    far_e = topo.engines(core, T.cores[far[0]])
    near_e = [e for e in topo.engines(core, T.cores[others[0]]) if e not in far_e]

    Q = {"v": g.vector, "t": g.tensor, "s": g.scalar, "p": g, "y": g.sync}
    cnt = {"v": 0, "t": 0, "s": 0, "p": 0}
    seen = {}

    def need(q, *toks):
        for s, n in toks:
            if seen.get((q, s), 0) < n:
                Q[q].wait_ge(T.sem[s], n)
                seen[(q, s)] = n

    def done(q, ins):
        ins.then_inc(T.sem[q], 1)
        cnt[q] += 1
        return (q, cnt[q])

    V, S, PE = g.vector, g.scalar, g.tensor
    v = lambda ins: done("v", ins)
    s = lambda ins: done("s", ins)
    t = lambda ins: done("t", ins)
    p = lambda ins: done("p", ins)
    ts = lambda out, in0, s1, s2, *ops: v(V.tensor_scalar(out, in0, s1, s2, *ops))
    tt = lambda out, a, b, op: v(V.tensor_tensor(out, a, b, op))

    g.sync.dma_start(T.wgs[:], T.wg[:, 0:32]).then_inc(T.sem.dwg, 16)
    g.scalar.dma_start(T.xs[:, 512:1024], T.x[:, 512:1024]).then_inc(T.sem.dx, 16)
    g.sync.dma_start(T.xs[:, 0:512], T.x[:, 0:512]).then_inc(T.sem.dx, 16)
    g.sync.dma_start(T.w1s[:], T.w1[:]).then_inc(T.sem.dw, 16)
    DWG, DX, DW = ("dwg", 16), ("dx", 32), ("dw", 16)

    imp = dict(allow_small_or_imprecise_dtypes=True)
    p_ic = p(g.iota(T.ic[:], [[0, 1]], 0, 1))
    for k, e in enumerate(X[0] + X[1]):
        p_e4 = p(g.iota(T.e4[:, 8 * k:8 * k + 8], [[0, 8]], 4 * e, 0, **imp))
    p_tok = p(g.iota(T.tok0[:], [[32, 8], [1, 16]], 0, 0, **imp))
    p_ib = p(g.iota(T.ib[:], [[1, 256]], 128, -1))
    v_ones = v(V.memset(T.ones[:], 1.0))
    need("p", v_ones)
    p_z = p(g.affine_select(T.z[:], T.ones[:], [[-1, 516]], A.is_equal, 0.0, 3, 4))
    p_id = p(g.iota(T.idr[:], [[W4, N], [4, CK]], 16, 0, **imp))

    need("v", p_ic)
    v_p3 = ts(T.p3[:], T.ic[:], 3, None, A.bitwise_and)
    v_h16i = ts(T.h16i[:], T.ic[:], 16, None, A.bitwise_and)
    v_q12 = ts(T.q12[:], T.ic[:], 12, None, A.bitwise_and)
    need("v", v_p3)
    v_p3f = ts(T.p3f[:], T.p3[:], 1.0, None, A.mult)
    need("v", v_h16i)
    v_h16 = ts(T.h16[:], T.h16i[:], 1.0, None, A.mult)
    need("v", v_p3f, p_e4)
    v_go = ts(T.go[:], T.e4[:], T.p3f[:, 0:1], None, A.add)
    v_d1 = v(V.memset(T.d0cnt[:], 1.0))
    need("v", DWG, v_go)
    v_gt = v(V.tensor_copy(T.gt0[:, 0:256], T.wgs[:, 0:32].indirect(T.go[:, 0:16])))
    need("s", DWG, v_go)
    s_gt0 = s(S.activation(T.gt0[:, 256:512], T.wgs[:, 0:32].indirect(T.go[:, 16:32]), F.Copy))
    s_gt1 = s(S.activation(T.gt1[:], T.wgs[:, 0:32].indirect(T.go[:, 32:64]), F.Copy))
    need("v", v_gt, s_gt0)
    v_gq = [v(V.quantize_mx(T.gq0[:, 0:128], T.gc0[:, 0:128], T.gt0[:, 0:512])), None]

    need("v", DX)
    v_xq = v(V.quantize_mx(T.xq[:, 0:256], T.xc[:, 0:256], T.xs[:, 0:1024]))
    v_z = [v(V.memset(T["ac%d" % h][:, 7:8], 0.0)) for h in range(2)]
    plane = lambda k: (T.xp[:, 256 * k:256 * k + 256], T.xs[:, k:1024:4])
    v_xp = v(V.tensor_copy(*plane(3)))
    need("s", DX)
    s(S.activation(*plane(0), F.Copy))
    sv, ss = [T.ps4, T.ps6], [T.ps5, T.ps7]
    t_sv, t_ss = [None, None], [None, None]

    def score(h):
        need("t", v_xq, v_gq[h])
        mm = lambda out: t(PE.matmul_mx(out, T["gq%d" % h][:, 0:128], T["gc%d" % h][:, 0:128], T.xq[:, 0:256], T.xc[:, 0:256], True, True))
        t_sv[h] = mm(sv[h][:, 0:256])
        t_ss[h] = mm(ss[h][:, 0:256])

    s_cnt, v_cnt, v_es, v_svread = [None, None], [None, None], [None, None], [None, None]
    const = {}

    def count(h):
        P, own, cm, PS, sg, ac = sv[h], T["tt%d" % h], T["cmp%d" % h], ss[h], T["sg%d" % h], T["ac%d" % h]
        need("v", t_sv[h])
        v_tt = v(V.transpose(own[:], P[:, 0:256]))
        need("s", t_ss[h], v_tt, v_z[h])
        sgn = [s(S.activation(sg[:, 256 * u:256 * u + 256], PS[:, 0:256], F.Sign, bias=own[:, 32 * b:32 * b + 1], scale=-1.0)) for u, b in enumerate(SB)]
        for u, b in enumerate(SB):
            need("s", sgn[u])
            m = 256 * u + 32 * (b + 1)
            lo = sg[:, 256 * u:m]
            s_cnt[h] = s(S.activation(lo, lo, F.Sign, bias=1.0, scale=-2.0, accum_out=ac[:, u:u + 1]))
            if b < 7:
                hi = sg[:, m:256 * u + 256]
                s_cnt[h] = s(S.activation(hi, hi, F.Sign, bias=-1.0, scale=-2.0, accum_out=ac[:, NS + u:NS + u + 1]))
        need("v", v_tt)
        v_eq = tt(T["eqb%d" % h][:], P[:, 0:256], own[:], A.is_equal)
        for u, b in enumerate(VB):
            m = 32 * (b + 1)
            ts(cm[:, 256 * u:256 * u + m], P[:, 0:m], own[:, 32 * b:32 * b + 1], None, A.is_ge)
            v_svread[h] = ts(cm[:, 256 * u + m:256 * u + 256], P[:, m:256], own[:, 32 * b:32 * b + 1], None, A.is_gt)
        if h == 0:
            need("v", v_d1, p_ib)
            v_ibm = ts(T.ibm[:], T.ib[:], 31, None, A.bitwise_and)
            const["d0"] = v(V.memset(T.d0cnt[:, 0:256 * NV:256], 0.0))
            need("v", v_ibm)
            const["blk"] = ts(T.d0blk[:], T.ibm[:], 0, None, A.not_equal)
            need("v", s_gt1)
            v_gq[1] = v(V.quantize_mx(T.gq1[:, 0:128], T.gc1[:, 0:128], T.gt1[:, 0:512]))
        need("v", v_svread[h], const["d0"])
        v_cnt[h] = v(V.tensor_tensor_scan(T["cs%d" % h][:], T.d0cnt[:], cm[:], 0.0, A.mult, A.add))
        need("v", v_eq, const["blk"])
        v_es[h] = v(V.tensor_tensor_scan(T["es%d" % h][:], T.d0blk[:], T["eqb%d" % h][:], 0.0, A.mult, A.add))
        if h == 0:
            need("v", p_tok, v_h16)
            const["tok"] = ts(T.tokv[:], T.tok0[:], T.h16[:, 0:1], None, A.add)
            const["wn"] = [v(V.memset(T["wn%d" % k][:, 0:CK], 0.0)) for k in range(2)]

    def invert(h, queues):
        B = lambda n: T["%s%d" % (n, h)]
        need("v", v_cnt[h], v_es[h])
        tt(B("rk")[:, 0:NV], B("cs")[:, 255:256 * NV:256], B("es")[:, 31:32 * NV:32], A.subtract)
        need("v", s_cnt[h])
        x2 = tt(B("a2")[:, 0:NS], B("ac")[:, 0:NS], B("ac")[:, NS:2 * NS], A.add)
        need("v", x2)
        x3 = ts(B("a3")[:, 0:NS], B("a2")[:, 0:NS], 0.5, 128.0, A.mult, A.add)
        need("v", x3)
        r2 = tt(B("rk")[:, NV:8], B("a3")[:, 0:NS], B("es")[:, 32 * NV + 31:256:32], A.subtract)
        need("v", r2)
        ru = ts(B("ru")[:, 0:8], B("rk")[:, 0:8], 1.0, None, A.mult)
        need("v", ru, const["tok"], const["wn"][h])
        w = v(V.tensor_copy(B("wn")[:, 0:256].indirect(B("ru")[:, 0:8]), T.tokv[:, 0:128]))
        for k in range(8):
            a, half, q = k // 2, k % 2, queues[k % len(queues)]
            need(q, w)
            lst = B("wn")[32 * a + 16 * half:32 * a + 16 * half + 8, 0:CK]
            Q[q].dma_start(B("lb" if half else "la")[:, 3 * a:3 * a + 3], lst).then_inc(T.sem["lo%d" % h], 16)

    v_of, v_ob = [None, None], [None, None]

    def pick(h, qbuf, cbuf):
        xg, of = T["xg%d" % h], T["of%d" % h]
        need("v", ("lo%d" % h, 128))
        v_ob[h] = tt(T["ob%d" % h][:], T["la%d" % h][:], T["lb%d" % h][:], A.add)
        need("v", v_ob[h])
        v_of[h] = ts(of[:], T["ob%d" % h][:], 1.0, None, A.mult)
        gat = lambda k: (xg[:, k:4 * W4:4], T.xp[:, 256 * k:256 * k + 256].indirect(of[:, 0:12]))
        need("s", s_xp, v_xp, v_of[h])
        need("v", s_xp, v_xp, v_of[h])
        for k in (0, 1):
            s_g = s(S.activation(*gat(k), F.Copy))
        for k in (2, 3):
            v_g = v(V.tensor_copy(*gat(k)))
        need("v", s_g, v_g)
        return v(V.quantize_mx(qbuf, cbuf, xg[:, 0:4 * W4]))

    ls = [0]

    def send(parts):
        for z in ("q", "c"):
            tr = []
            for d, src, a, dst, b, sem in parts:
                rid, pid, _ = topo.addr(T.cores[d])
                k, eng = (far.index(d), far_e) if d in far else (others.index(d), near_e)
                sa, da = T[src + z][:, a:a + CK], T[dst + z][:, b:b + CK]
                if z == "q":
                    sa, da = sa.bitcast(dt.uint8), da.bitcast(dt.uint8)
                tr.append(RemoteDMATransfer(dst_ids=[DstId(rid=rid, pnc=pid)], dma_engine_mask=(1 << eng[2 * k]) | (1 << eng[2 * k + 1]),
                                            remote_sem=T.sem[sem], src=sa, dst=da))
                ls[0] += 2
            g.remote_dma_fused(tr, local_sem=T.sem.ls)

    in_far = lambda d: CK * far_of(d).index(rank)
    in_near = lambda d: CK * near_of(d).index(rank)

    def dispatch(h):
        src = "t" if kind[h] == "far" else "n"
        x = pick(h, T[src + "q"][:, 0:W4], T[src + "c"][:, 0:W4])
        need("p", x)
        if kind[h] == "far":
            send([(d, "t", CK * k, "n", 336 + in_far(d), "af") for k, d in enumerate(far)])
        else:
            send([(d, "n", CK * k, "n", W4 + in_near(d), "an") for k, d in enumerate(others)])
        return x

    table = T.pl[:, 384:640]
    v_chain = [None, None]

    def chain(h):
        need("v", v_ob[h])
        for m in range(3):
            x = ts(T["ol%d" % h][:, m:16:4], T["ob%d" % h][:, m:12:3], 1.0, None, A.mult)
        need("v", x, v_fresh, p_id)
        for e in sorted(X[h]):
            a = where[e][1]
            at = table.indirect(T["ol%d" % h][:, 4 * a:4 * a + 3])
            o = W4 * h + CK * a
            if e == 0:
                x = v(V.memset(T.pl[:, o:o + CK], 0.0))
            else:
                x = v(V.tensor_copy(T.pl[:, o:o + CK], at))
            need("v", x)
            x = v(V.tensor_copy(at, T.idr[:, CK * e:CK * e + CK]))
            need("v", x)
        v_chain[h] = x

    score(0)
    count(0)
    score(1)
    for k in (1, 2):
        s_xp = s(S.activation(*plane(k), F.Copy))
    invert(0, ["y"])
    count(1)
    invert(1, ["y", "s"])
    v_x = [dispatch(0), None]
    need("v", DW)
    v_wq = v(V.quantize_mx(T.wq[:, 0:512], T.wc[:, 0:512], T.w1s[:, 0:2048]))
    v_fresh = v(V.memset(table, 0.0))
    v_x[1] = dispatch(1)
    chain(0)
    chain(1)
    need("v", p_z)
    for b in range(4):
        v_ebq = v(V.quantize_mx(T.eq[:, 128 * b:128 * b + 128], T.ec[:, 128 * b:128 * b + 128], T.z[:, 3 - b:515 - b]))

    def addresses():
        need("v", v_q12)
        for k in range(4):
            v_mk = ts(T.mk[:, k:k + 1], T.q12[:], float(4 * k), None, A.is_equal)
        v(V.memset(T.pb[:, 0:16], 0.0))
        need("s", v_chain[1], v_mk)
        dg = [T["dg%d" % k] for k in range(4)]
        for k in range(4):
            s_dg = s(S.activation(dg[k][:], T.pl[:, k:640:4], F.Identity, scale=T.mk[:, k:k + 1]))
        need("v", s_dg)
        tt(T.d01[:], dg[0][:], dg[1][:], A.add)
        need("v", tt(T.d23[:], dg[2][:], dg[3][:], A.add))
        need("v", tt(T.dd[:], T.d01[:], T.d23[:], A.add))
        return ts(T.op[:], T.dd[:], T.p3f[:, 0:1], None, A.add)

    def expert():
        need("t", v_wq, v_x[kind.index("near")], ("an", 12), ("af", 16))
        W8 = 2 * W4
        tm = [t(PE.matmul_mx(T["ps%d" % i][:, 0:W8], T.wq[:, 128 * i:128 * i + 128], T.wc[:, 128 * i:128 * i + 128],
                             T.nq[:, 144:528], T["nc"][:, 144:528], True, True)) for i in range(4)]
        for i in (0, 2):
            need("s", tm[i])
            s_r = s(S.activation(T.hh[:, i:4 * W8:4], T["ps%d" % i][:, 0:W8], F.Relu, scale=0.05))
            need("v", tm[i + 1])
            v_r = ts(T.hh[:, i + 1:4 * W8:4], T["ps%d" % (i + 1)][:, 0:W8], 0.0, 0.05, A.max, A.mult)
        need("v", s_r, v_r)
        x = v(V.quantize_mx(T.mq[:, 144:528], T.mc[:, 144:528], T.hh[:, 0:4 * W8]))
        need("p", x)
        send([(d, "m", 336 + CK * k, "m", 528 + in_far(d), "rf") for k, d in enumerate(far)]
             + [(d, "m", W4 + CK * k, "m", in_near(d), "rn") for k, d in enumerate(others)])
        return x, [s_r, v_r]

    v_h, free = expert()
    v_op = addresses()

    def unpack(pieces, banks, qv, cv, ready):
        need("t", v_ebq, *ready)
        tm = [t(PE.matmul_mx(T["ps%d" % k][:, 0:W4], T.eq[:, 128 * b:128 * b + 128], T.ec[:, 128 * b:128 * b + 128], qv, cv, True, True)) for b, k in enumerate(banks)]
        for b in (0, 2):
            for q, f in (("s", b), ("v", b + 1)):
                need(q, tm[f])
                for lo, hi, buf, at in pieces:
                    o, i = buf[:, 4 * at + f:4 * (at + hi - lo):4], T["ps%d" % banks[f]][:, lo:hi]
                    if q == "s":
                        s_r = s(S.activation(o, i, F.Copy))
                    else:
                        v_r = v(V.tensor_copy(o, i))
        return [s_r, v_r]

    for c in range(2):
        ds = T["ds%d" % c]
        pieces = [(0, W4, ds, 0)]
        if c == 0:
            z = CK * where[0][1]
            pieces = [(z, z + CK, T.pb, 4)] + [(lo, hi, ds, lo) for lo, hi in ((0, z), (z + CK, W4)) if lo < hi]
        if kind[c] == "far":
            ready = unpack(pieces, [0, 1, 2, 3], T.mq[:, 528:720], T.mc[:, 528:720], [("rf", 16)] + free)
        else:
            ready = unpack(pieces, [4, 5, 6, 7], T.mq[:, 0:W4], T.mc[:, 0:W4], [("rn", 12), v_h, v_svread[1], s_cnt[1]])
        need("v", v_op, *ready)
        for e in sorted(X[c]):
            if e == 0:
                continue
            d, o, k = W4 * where[e][1], 16 + W4 * e, 48 * c + 12 * where[e][1]
            x = tt(T.pb[:, o:o + W4], T.pb[:, 0:o].indirect(T.op[:, k:k + 12]), ds[:, d:d + W4], A.add)
            need("v", x)
    win = T.pb[:, 0:16 + N * W4]
    need("s", x)
    s_y = s(S.activation(T.yt[:, 512:1024], win.indirect(T.op[:, 128:160]), F.Copy))
    v_y = v(V.tensor_copy(T.yt[:, 0:512], win.indirect(T.op[:, 96:128])))
    need("y", v_y)
    g.sync.dma_start(T.y[:, 0:512], T.yt[:, 0:512]).then_inc(T.sem.dy, 16)
    need("s", s_y)
    g.scalar.dma_start(T.y[:, 512:1024], T.yt[:, 512:1024]).then_inc(T.sem.dy, 16)

    need("p", ("ls", ls[0]), ("dwg", 16), DX, DW, ("lo0", 128), ("lo1", 128), ("af", 16), ("an", 12), ("rf", 16), ("rn", 12), ("dy", 32))
    need("p", *[(q, cnt[q]) for q in ("v", "s", "t", "p")])
